import numpy as np, ml_dtypes
CORES = [12,28,44,60,3,19,35,51]
N = 8
T, CAP = 2048, 128
def entries(a): return a.T.reshape(-1)
def pack(v, P): return np.ascontiguousarray(np.asarray(v, np.int32).reshape(-1, P).T)
def lists(rng, how):
    L = rng.integers(0, T, (N, N, CAP))
    if how == "alike": L[:] = rng.integers(0, T, (N, N, 1))
    if how == "distinct": L = np.stack([np.stack([rng.permutation(T)[:CAP] for d in range(N)]) for r in range(N)])
    if how == "sorted": L = np.sort(L, axis=2)
    if how == "edge": L = np.where(rng.random((N, N, CAP)) < 0.5, 0, T - 1)
    return {"l": np.stack([pack(L[r].reshape(-1), 16) for r in range(N)])}
def setup_inputs(rng):
    return dict({"x": rng.standard_normal((N, 128, T), dtype=np.float32).astype(ml_dtypes.bfloat16)}, **lists(rng, "uniform"))
def setup_inputs_alike(rng):
    d = setup_inputs(rng); d.update(lists(rng, "alike"))
    for k in ("x",): d[k] = (d[k].astype(np.float32) * 1048576.0).astype(d[k].dtype)
    return d
def setup_inputs_distinct(rng):
    d = setup_inputs(rng); d.update(lists(rng, "distinct"))
    for k in ("x",): d[k] = (d[k].astype(np.float32) * (1 / 1024.0)).astype(d[k].dtype)
    return d
def setup_inputs_edge(rng):
    d = setup_inputs(rng); d.update(lists(rng, "edge"))
    return d
def setup_inputs_sorted(rng):
    d = setup_inputs(rng); d.update(lists(rng, "sorted"))
    return d
def check_inputs(x):
    bad = []
    if x["l"].min() < 0 or x["l"].max() >= T: bad.append("l out of range")
    return bad
def reference(x, l):
    y = np.zeros((N, 128, N * CAP), x.dtype)
    for r in range(N):
        L = entries(l[r])
        for d in range(N): y[d][:, CAP * r:CAP * r + CAP] = x[r][:, L[CAP * d:CAP * d + CAP]]
    return {"y": y}

@@ -1,0 +1,169 @@
+from concourse.bass import DstId, RemoteDMATransfer
+from concourse.mybir import AluOpType
+
+SIM_CORES = 64
+CAP = 128
+COLS = 2048
+LROWS = 16
+LW = CAP // LROWS
+
+SCRATCH = {
+    "xs": ("sbuf", [128, COLS], "bfloat16"),
+    "snd": ("sbuf", [128, 8 * CAP], "bfloat16"),
+    "land": ("sbuf", [128, 8 * CAP], "bfloat16"),
+    "hold": ("sbuf", [128, CAP], "bfloat16"),
+    "lraw": ("sbuf", [128, 8 * LW], "int32"),
+    "lf": ("sbuf", [128, 8 * LW], "float32"),
+    "ramp": ("sbuf", [128, 128], "float32"),
+    "rep": ("sbuf", [128, 128], "float32"),
+    "off": ("sbuf", [128, 8 * LW], "uint16"),
+    "ps": ("psum", [128, 8 * LW], "float32"),
+}
+SEMAPHORES = ["lin", "xin", "c0", "c1", "c2", "c3", "gs0", "gs1", "gs2", "gs3", "own",
+              "fed", "sent", "lo", "hi", "stlo", "sthi"]
+
+
+def _bits(mask):
+    return [b for b in range(mask.bit_length()) if (mask >> b) & 1]
+
+
+def _mask(bits):
+    m = 0
+    for b in bits:
+        m |= 1 << b
+    return m
+
+
+def _split(bits, k):
+    w = len(bits) // k
+    return [bits[i * w:(i + 1) * w] for i in range(k)]
+
+
+def _half(r, n):
+    return "lo" if r < n // 2 else "hi"
+
+
+def _plan(T, topo):
+    cores = list(T.cores)
+    n = len(cores)
+    calls = {}
+    jobs = {}
+    arrive = {d: {"lo": 0, "hi": 0} for d in range(n)}
+    for r, c in enumerate(cores):
+        ch = topo.chip(c)
+        near = [d for d in range(n) if d != r and topo.same_plane(ch, topo.chip(cores[d]))]
+        cross = [d for d in range(n) if d != r and d not in near]
+        m = [i for i, d in enumerate(cross) if topo.mates(ch, topo.chip(cores[d]))][0]
+        cross = cross[m:] + cross[:m]
+        i = len([d for d in near if d < r])
+        near = near[i:] + near[:i]
+        free = [h for h in range(SIM_CORES) if topo.chip(h) == ch and T.rank_of(h) is None]
+        ports = [h for h in free if all(topo.may_write(h, cores[d]) for d in cross)]
+        ports.sort(key=lambda h: topo.die(h) != topo.die(cores[cross[0]]))
+        relay = list(zip(cross, ports))
+        direct = cross[len(relay):] + near
+        away = _bits(topo.mask(c, cores[near[0]]))
+        home = [b for b in _bits(topo.mask(c, ports[0])) if b not in away]
+        mine = []
+        for part, eng in ((relay[-2:], home), (relay[:-2], away)):
+            mine.append([(d, h, True, e) for (d, h), e in zip(part, _split(eng, len(part)))])
+        rest = list(direct)
+        while rest:
+            k = 4 if len(rest) >= 4 else 2 if len(rest) >= 2 else 1
+            mine.append([(d, cores[d], False, e) for d, e in zip(rest[:k], _split(away, k))])
+            rest = rest[k:]
+        calls[r] = mine
+        for call in mine:
+            for d, tgt, feed, e in call:
+                if feed:
+                    jobs[tgt] = (r, d, len(e))
+                    arrive[d][_half(r, n)] += len(_bits(topo.mask(tgt, cores[d])))
+                else:
+                    arrive[d][_half(r, n)] += len(e)
+    return calls, jobs, arrive
+
+
+def _runs(ds):
+    out = []
+    for d in sorted(ds):
+        if out and out[-1][1] == d:
+            out[-1][1] = d + 1
+        else:
+            out.append([d, d + 1])
+    return out
+
+
+def rank_program(g, core, T, topo):
+    calls, jobs, arrive = _plan(T, topo)
+    S = T.sem
+    n = len(T.cores)
+
+    if core in jobs:
+        r, d, fed = jobs[core]
+        dst = T.cores[d]
+        rid, pid, _se = topo.addr(dst)
+        m = topo.mask(core, dst)
+        g.wait_ge(S.fed, fed)
+        g.remote_dma(T.land[:, CAP * r:CAP * (r + 1)], T.hold[:, :], S[_half(r, n)], S.sent, pid, rid, m)
+        g.wait_ge(S.sent, len(_bits(m)))
+        return
+
+    rank = T.rank_of(core)
+    if rank is None:
+        return
+    v = g.vector
+
+    g.sync.dma_start(T.lraw[0:LROWS, :], T.l[:, :]).then_inc(S.lin, 16)
+    g.scalar.dma_start(T.xs[0:64, :], T.x[0:64, :]).then_inc(S.xin, 16)
+    g.sync.dma_start(T.xs[64:128, :], T.x[64:128, :]).then_inc(S.xin, 16)
+
+    g.iota(T.ramp[0:LROWS, :], [[0, 128 // LROWS], [1, LROWS]], 0, -1,
+           allow_small_or_imprecise_dtypes=True).then_inc(S.c0, 1)
+    v.wait_ge(S.c0, 1)
+    v.tensor_scalar(T.rep[0:LROWS, :], T.ramp[0:LROWS, :], 0.0, None, AluOpType.is_equal).then_inc(S.c1, 1)
+    v.wait_ge(S.lin, 16)
+    v.tensor_copy(T.lf[0:LROWS, :], T.lraw[0:LROWS, :]).then_inc(S.c1, 1)
+    g.tensor.wait_ge(S.c1, 2)
+    g.tensor.matmul(T.ps[:, :], T.rep[0:LROWS, :], T.lf[0:LROWS, :], True, True).then_inc(S.c2, 1)
+    v.wait_ge(S.c2, 1)
+    v.tensor_copy(T.off[:, :], T.ps[:, :]).then_inc(S.c3, 1)
+    v.wait_ge(S.c3, 1)
+    v.wait_ge(S.xin, 32)
+
+    mine = calls[rank]
+    nruns = []
+    for k, call in enumerate(mine):
+        runs = _runs([t[0] for t in call])
+        nruns.append(len(runs))
+        for a, b in runs:
+            v.tensor_copy(T.snd[:, CAP * a:CAP * b],
+                          T.xs[:, 0:COLS].indirect(T.off[:, LW * a:LW * b])).then_inc(S["gs%d" % k], 1)
+    v.tensor_copy(T.land[:, CAP * rank:CAP * (rank + 1)],
+                  T.xs[:, 0:COLS].indirect(T.off[:, LW * rank:LW * (rank + 1)])).then_inc(S.own, 1)
+
+    sent = 0
+    for k, call in enumerate(mine):
+        g.wait_ge(S["gs%d" % k], nruns[k])
+        trs = []
+        for d, tgt, feed, eng in call:
+            rid, pid, _se = topo.addr(tgt)
+            out = T.hold[:, :] if feed else T.land[:, CAP * rank:CAP * (rank + 1)]
+            sem = S.fed if feed else S[_half(rank, n)]
+            src = T.snd[:, CAP * d:CAP * (d + 1)]
+            sent += len(eng)
+            if len(call) == 1:
+                g.remote_dma(out, src, sem, S.sent, pid, rid, _mask(eng))
+            else:
+                trs.append(RemoteDMATransfer(dst_ids=[DstId(rid=rid, pnc=pid)], dma_engine_mask=_mask(eng),
+                                             remote_sem=sem, src=src, dst=out))
+        if trs:
+            g.remote_dma_fused(trs, local_sem=S.sent)
+
+    w = CAP * n // 2
+    for i, (name, q, done) in enumerate((("lo", g.sync, "stlo"), ("hi", g.scalar, "sthi"))):
+        if _half(rank, n) == name:
+            q.wait_ge(S.own, 1)
+        q.wait_ge(S[name], arrive[rank][name])
+        q.dma_start(T.y[:, w * i:w * (i + 1)], T.land[:, w * i:w * (i + 1)]).then_inc(S[done], 16)
+        q.wait_ge(S[done], 16)
+    g.wait_ge(S.sent, sent)

@@ -1,5 +1,5 @@
 from concourse.bass import DstId, RemoteDMATransfer
-from concourse.mybir import AluOpType
+from concourse.mybir import AluOpType, ActivationFunctionType
 
 SIM_CORES = 64
 CAP = 128
@@ -11,7 +11,8 @@ SCRATCH = {
     "xs": ("sbuf", [128, COLS], "bfloat16"),
     "snd": ("sbuf", [128, 8 * CAP], "bfloat16"),
     "land": ("sbuf", [128, 8 * CAP], "bfloat16"),
-    "hold": ("sbuf", [128, CAP], "bfloat16"),
+    "hold0": ("sbuf", [128, CAP], "bfloat16"),
+    "hold1": ("sbuf", [128, CAP], "bfloat16"),
     "lraw": ("sbuf", [128, 8 * LW], "int32"),
     "lf": ("sbuf", [128, 8 * LW], "float32"),
     "ramp": ("sbuf", [128, 128], "float32"),
@@ -19,8 +20,8 @@ SCRATCH = {
     "off": ("sbuf", [128, 8 * LW], "uint16"),
     "ps": ("psum", [128, 8 * LW], "float32"),
 }
-SEMAPHORES = ["lin", "xin", "c0", "c1", "c2", "c3", "gs0", "gs1", "gs2", "gs3", "own",
-              "fed", "sent", "lo", "hi", "stlo", "sthi"]
+SEMAPHORES = (["lin", "xin", "c0", "c1", "c2", "c3", "fed0", "fed1", "sent", "stn", "stc"]
+              + ["q%d" % d for d in range(8)] + ["a%d" % r for r in range(8)])
 
 
 def _bits(mask):
@@ -34,87 +35,77 @@ def _mask(bits):
     return m
 
 
-def _split(bits, k):
-    w = len(bits) // k
-    return [bits[i * w:(i + 1) * w] for i in range(k)]
-
-
-def _half(r, n):
-    return "lo" if r < n // 2 else "hi"
-
-
 def _plan(T, topo):
     cores = list(T.cores)
     n = len(cores)
     calls = {}
+    picks = {}
     jobs = {}
-    arrive = {d: {"lo": 0, "hi": 0} for d in range(n)}
+    nearq = {d: {} for d in range(n)}
+    crossq = {d: {} for d in range(n)}
     for r, c in enumerate(cores):
         ch = topo.chip(c)
         near = [d for d in range(n) if d != r and topo.same_plane(ch, topo.chip(cores[d]))]
         cross = [d for d in range(n) if d != r and d not in near]
         m = [i for i, d in enumerate(cross) if topo.mates(ch, topo.chip(cores[d]))][0]
-        cross = cross[m:] + cross[:m]
+        rot = cross[m:] + cross[:m]
+        cross = [rot[1], rot[2], rot[0], rot[3]]
         i = len([d for d in near if d < r])
         near = near[i:] + near[:i]
         free = [h for h in range(SIM_CORES) if topo.chip(h) == ch and T.rank_of(h) is None]
         ports = [h for h in free if all(topo.may_write(h, cores[d]) for d in cross)]
-        ports.sort(key=lambda h: topo.die(h) != topo.die(cores[cross[0]]))
-        relay = list(zip(cross, ports))
-        direct = cross[len(relay):] + near
+        rdie = topo.die(cores[rot[0]])
+        hx = [h for h in ports if topo.die(h) != rdie][0]
+        ha, hb = [h for h in ports if topo.die(h) == rdie][:2]
         away = _bits(topo.mask(c, cores[near[0]]))
-        home = [b for b in _bits(topo.mask(c, ports[0])) if b not in away]
-        mine = []
-        for part, eng in ((relay[-2:], home), (relay[:-2], away)):
-            mine.append([(d, h, True, e) for (d, h), e in zip(part, _split(eng, len(part)))])
-        rest = list(direct)
-        while rest:
-            k = 4 if len(rest) >= 4 else 2 if len(rest) >= 2 else 1
-            mine.append([(d, cores[d], False, e) for d, e in zip(rest[:k], _split(away, k))])
-            rest = rest[k:]
-        calls[r] = mine
-        for call in mine:
-            for d, tgt, feed, e in call:
-                if feed:
-                    jobs[tgt] = (r, d, len(e))
-                    arrive[d][_half(r, n)] += len(_bits(topo.mask(tgt, cores[d])))
-                else:
-                    arrive[d][_half(r, n)] += len(e)
-    return calls, jobs, arrive
-
-
-def _runs(ds):
-    out = []
-    for d in sorted(ds):
-        if out and out[-1][1] == d:
-            out[-1][1] = d + 1
-        else:
-            out.append([d, d + 1])
-    return out
+        home = [b for b in _bits(topo.mask(c, hx)) if b not in away]
+        ea, eb = home[0::2], home[1::2]
+        wa, wb = away[0::2], away[1::2]
+        calls[r] = [
+            [(cross[0], ha, 0, ea)],
+            [(cross[1], hx, 0, eb)],
+            [(cross[2], hb, 0, ea), (cross[3], hx, 1, eb)],
+            [(near[0], cores[near[0]], None, wa), (near[1], cores[near[1]], None, wb)],
+            [(near[2], cores[near[2]], None, away)],
+        ]
+        hl = LW // 2
+        picks[r] = ([(cross[0], 0, hl), (cross[1], 0, hl), (cross[2], 0, LW), (near[0], 0, LW), (near[2], 0, LW)],
+                    [(cross[0], hl, LW), (cross[1], hl, LW), (cross[3], 0, LW), (near[1], 0, LW), (r, 0, LW)])
+        jobs[ha] = (r, [(cross[0], len(ea))])
+        jobs[hx] = (r, [(cross[1], len(eb)), (cross[3], len(eb))])
+        jobs[hb] = (r, [(cross[2], len(ea))])
+        for k, (d, e) in enumerate(zip(near, (wa, wb, away))):
+            nearq[d][k] = (r, len(e))
+        for k, (d, h) in enumerate(zip(cross, (ha, hx, hb, hx))):
+            crossq[d][k] = (r, len(_bits(topo.mask(h, cores[d]))))
+    return calls, picks, jobs, nearq, crossq
 
 
 def rank_program(g, core, T, topo):
-    calls, jobs, arrive = _plan(T, topo)
+    calls, picks, jobs, nearq, crossq = _plan(T, topo)
     S = T.sem
-    n = len(T.cores)
 
     if core in jobs:
-        r, d, fed = jobs[core]
-        dst = T.cores[d]
-        rid, pid, _se = topo.addr(dst)
-        m = topo.mask(core, dst)
-        g.wait_ge(S.fed, fed)
-        g.remote_dma(T.land[:, CAP * r:CAP * (r + 1)], T.hold[:, :], S[_half(r, n)], S.sent, pid, rid, m)
-        g.wait_ge(S.sent, len(_bits(m)))
+        r, work = jobs[core]
+        sent = 0
+        for k, (d, fed) in enumerate(work):
+            dst = T.cores[d]
+            rid, pid, _se = topo.addr(dst)
+            m = topo.mask(core, dst)
+            g.wait_ge(S["fed%d" % k], fed)
+            g.remote_dma(T.land[:, CAP * r:CAP * (r + 1)], T["hold%d" % k][:, :], S["a%d" % r], S.sent, pid, rid, m)
+            sent += len(_bits(m))
+        g.wait_ge(S.sent, sent)
         return
 
     rank = T.rank_of(core)
     if rank is None:
         return
     v = g.vector
+    sc = g.scalar
 
     g.sync.dma_start(T.lraw[0:LROWS, :], T.l[:, :]).then_inc(S.lin, 16)
-    g.scalar.dma_start(T.xs[0:64, :], T.x[0:64, :]).then_inc(S.xin, 16)
+    sc.dma_start(T.xs[0:64, :], T.x[0:64, :]).then_inc(S.xin, 16)
     g.sync.dma_start(T.xs[64:128, :], T.x[64:128, :]).then_inc(S.xin, 16)
 
     g.iota(T.ramp[0:LROWS, :], [[0, 128 // LROWS], [1, LROWS]], 0, -1,
@@ -127,28 +118,36 @@ def rank_program(g, core, T, topo):
     g.tensor.matmul(T.ps[:, :], T.rep[0:LROWS, :], T.lf[0:LROWS, :], True, True).then_inc(S.c2, 1)
     v.wait_ge(S.c2, 1)
     v.tensor_copy(T.off[:, :], T.ps[:, :]).then_inc(S.c3, 1)
-    v.wait_ge(S.c3, 1)
-    v.wait_ge(S.xin, 32)
 
-    mine = calls[rank]
-    nruns = []
-    for k, call in enumerate(mine):
-        runs = _runs([t[0] for t in call])
-        nruns.append(len(runs))
-        for a, b in runs:
-            v.tensor_copy(T.snd[:, CAP * a:CAP * b],
-                          T.xs[:, 0:COLS].indirect(T.off[:, LW * a:LW * b])).then_inc(S["gs%d" % k], 1)
-    v.tensor_copy(T.land[:, CAP * rank:CAP * (rank + 1)],
-                  T.xs[:, 0:COLS].indirect(T.off[:, LW * rank:LW * (rank + 1)])).then_inc(S.own, 1)
+    def target(d, a, b):
+        buf = T.land if d == rank else T.snd
+        return buf[:, CAP * d + LROWS * a:CAP * d + LROWS * b]
+
+    def column(d, a, b):
+        return T.xs[:, 0:COLS].indirect(T.off[:, LW * d + a:LW * d + b])
+
+    for q in (v, sc):
+        q.wait_ge(S.c3, 1)
+        q.wait_ge(S.xin, 32)
+    byv, bys = picks[rank]
+    parts = {}
+    for d, a, b in byv + bys:
+        parts[d] = parts.get(d, 0) + 1
+    for d, a, b in byv:
+        v.tensor_copy(target(d, a, b), column(d, a, b)).then_inc(S["q%d" % d], 1)
+    for d, a, b in bys:
+        sc.activation(target(d, a, b), column(d, a, b), ActivationFunctionType.Copy,
+                      bias=-0.0, scale=1.0).then_inc(S["q%d" % d], 1)
 
     sent = 0
-    for k, call in enumerate(mine):
-        g.wait_ge(S["gs%d" % k], nruns[k])
+    for call in calls[rank]:
         trs = []
-        for d, tgt, feed, eng in call:
+        for d, tgt, slot, eng in call:
+            g.wait_ge(S["q%d" % d], parts[d])
+        for d, tgt, slot, eng in call:
             rid, pid, _se = topo.addr(tgt)
-            out = T.hold[:, :] if feed else T.land[:, CAP * rank:CAP * (rank + 1)]
-            sem = S.fed if feed else S[_half(rank, n)]
+            out = T.land[:, CAP * rank:CAP * (rank + 1)] if slot is None else T["hold%d" % slot][:, :]
+            sem = S["a%d" % rank] if slot is None else S["fed%d" % slot]
             src = T.snd[:, CAP * d:CAP * (d + 1)]
             sent += len(eng)
             if len(call) == 1:
@@ -159,11 +158,19 @@ def rank_program(g, core, T, topo):
         if trs:
             g.remote_dma_fused(trs, local_sem=S.sent)
 
-    w = CAP * n // 2
-    for i, (name, q, done) in enumerate((("lo", g.sync, "stlo"), ("hi", g.scalar, "sthi"))):
-        if _half(rank, n) == name:
-            q.wait_ge(S.own, 1)
-        q.wait_ge(S[name], arrive[rank][name])
-        q.dma_start(T.y[:, w * i:w * (i + 1)], T.land[:, w * i:w * (i + 1)]).then_inc(S[done], 16)
-        q.wait_ge(S[done], 16)
+    def store(q, r, done):
+        q.dma_start(T.y[:, CAP * r:CAP * (r + 1)], T.land[:, CAP * r:CAP * (r + 1)]).then_inc(S[done], 16)
+
+    nq = [nearq[rank][k] for k in sorted(nearq[rank])]
+    cq = [crossq[rank][k] for k in sorted(crossq[rank])]
+    g.sync.wait_ge(S["q%d" % rank], parts[rank])
+    store(g.sync, rank, "stn")
+    for r, cnt in nq + cq[:1]:
+        g.sync.wait_ge(S["a%d" % r], cnt)
+        store(g.sync, r, "stn")
+    g.sync.wait_ge(S.stn, 16 * (len(nq) + 2))
+    for r, cnt in cq[1:]:
+        sc.wait_ge(S["a%d" % r], cnt)
+        store(sc, r, "stc")
+    sc.wait_ge(S.stc, 16 * (len(cq) - 1))
     g.wait_ge(S.sent, sent)

from concourse.bass import DstId, RemoteDMATransfer
from concourse.mybir import AluOpType, ActivationFunctionType

SIM_CORES = 64
CAP = 128
COLS = 2048
LROWS = 16
LW = CAP // LROWS

SCRATCH = {
    "xs": ("sbuf", [128, COLS], "bfloat16"),
    "snd": ("sbuf", [128, 8 * CAP], "bfloat16"),
    "land": ("sbuf", [128, 8 * CAP], "bfloat16"),
    "hold0": ("sbuf", [128, CAP], "bfloat16"),
    "hold1": ("sbuf", [128, CAP], "bfloat16"),
    "lraw": ("sbuf", [128, 8 * LW], "int32"),
    "lf": ("sbuf", [128, 8 * LW], "float32"),
    "ramp": ("sbuf", [128, 128], "float32"),
    "rep": ("sbuf", [128, 128], "float32"),
    "off": ("sbuf", [128, 8 * LW], "uint16"),
    "ps": ("psum", [128, 8 * LW], "float32"),
}
SEMAPHORES = (["lin", "xin", "c0", "c1", "c2", "c3", "fed0", "fed1", "sent", "stn", "stc"]
              + ["q%d" % d for d in range(8)] + ["a%d" % r for r in range(8)])


def _bits(mask):
    return [b for b in range(mask.bit_length()) if (mask >> b) & 1]


def _mask(bits):
    m = 0
    for b in bits:
        m |= 1 << b
    return m


def _plan(T, topo):
    cores = list(T.cores)
    n = len(cores)
    calls = {}
    picks = {}
    jobs = {}
    nearq = {d: {} for d in range(n)}
    crossq = {d: {} for d in range(n)}
    for r, c in enumerate(cores):
        ch = topo.chip(c)
        near = [d for d in range(n) if d != r and topo.same_plane(ch, topo.chip(cores[d]))]
        cross = [d for d in range(n) if d != r and d not in near]
        m = [i for i, d in enumerate(cross) if topo.mates(ch, topo.chip(cores[d]))][0]
        rot = cross[m:] + cross[:m]
        cross = [rot[1], rot[2], rot[0], rot[3]]
        i = len([d for d in near if d < r])
        near = near[i:] + near[:i]
        free = [h for h in range(SIM_CORES) if topo.chip(h) == ch and T.rank_of(h) is None]
        ports = [h for h in free if all(topo.may_write(h, cores[d]) for d in cross)]
        rdie = topo.die(cores[rot[0]])
        hx = [h for h in ports if topo.die(h) != rdie][0]
        ha, hb = [h for h in ports if topo.die(h) == rdie][:2]
        away = _bits(topo.mask(c, cores[near[0]]))
        home = [b for b in _bits(topo.mask(c, hx)) if b not in away]
        ea, eb = home[0::2], home[1::2]
        wa, wb = away[0::2], away[1::2]
        calls[r] = [
            [(cross[0], ha, 0, ea)],
            [(cross[1], hx, 0, eb)],
            [(cross[2], hb, 0, ea), (cross[3], hx, 1, eb)],
            [(near[0], cores[near[0]], None, wa), (near[1], cores[near[1]], None, wb)],
            [(near[2], cores[near[2]], None, away)],
        ]
        hl = LW // 2
        picks[r] = ([(cross[0], 0, hl), (cross[1], 0, hl), (cross[2], 0, LW), (near[0], 0, LW), (near[2], 0, LW)],
                    [(cross[0], hl, LW), (cross[1], hl, LW), (cross[3], 0, LW), (near[1], 0, LW), (r, 0, LW)])
        jobs[ha] = (r, [(cross[0], len(ea))])
        jobs[hx] = (r, [(cross[1], len(eb)), (cross[3], len(eb))])
        jobs[hb] = (r, [(cross[2], len(ea))])
        for k, (d, e) in enumerate(zip(near, (wa, wb, away))):
            nearq[d][k] = (r, len(e))
        for k, (d, h) in enumerate(zip(cross, (ha, hx, hb, hx))):
            crossq[d][k] = (r, len(_bits(topo.mask(h, cores[d]))))
    return calls, picks, jobs, nearq, crossq


def rank_program(g, core, T, topo):
    calls, picks, jobs, nearq, crossq = _plan(T, topo)
    S = T.sem

    if core in jobs:
        r, work = jobs[core]
        sent = 0
        for k, (d, fed) in enumerate(work):
            dst = T.cores[d]
            rid, pid, _se = topo.addr(dst)
            m = topo.mask(core, dst)
            g.wait_ge(S["fed%d" % k], fed)
            g.remote_dma(T.land[:, CAP * r:CAP * (r + 1)], T["hold%d" % k][:, :], S["a%d" % r], S.sent, pid, rid, m)
            sent += len(_bits(m))
        g.wait_ge(S.sent, sent)
        return

    rank = T.rank_of(core)
    if rank is None:
        return
    v = g.vector
    sc = g.scalar

    g.sync.dma_start(T.lraw[0:LROWS, :], T.l[:, :]).then_inc(S.lin, 16)
    sc.dma_start(T.xs[0:64, :], T.x[0:64, :]).then_inc(S.xin, 16)
    g.sync.dma_start(T.xs[64:128, :], T.x[64:128, :]).then_inc(S.xin, 16)

    g.iota(T.ramp[0:LROWS, :], [[0, 128 // LROWS], [1, LROWS]], 0, -1,
           allow_small_or_imprecise_dtypes=True).then_inc(S.c0, 1)
    v.wait_ge(S.c0, 1)
    v.tensor_scalar(T.rep[0:LROWS, :], T.ramp[0:LROWS, :], 0.0, None, AluOpType.is_equal).then_inc(S.c1, 1)
    v.wait_ge(S.lin, 16)
    v.tensor_copy(T.lf[0:LROWS, :], T.lraw[0:LROWS, :]).then_inc(S.c1, 1)
    g.tensor.wait_ge(S.c1, 2)
    g.tensor.matmul(T.ps[:, :], T.rep[0:LROWS, :], T.lf[0:LROWS, :], True, True).then_inc(S.c2, 1)
    v.wait_ge(S.c2, 1)
    v.tensor_copy(T.off[:, :], T.ps[:, :]).then_inc(S.c3, 1)

    def target(d, a, b):
        buf = T.land if d == rank else T.snd
        return buf[:, CAP * d + LROWS * a:CAP * d + LROWS * b]

    def column(d, a, b):
        return T.xs[:, 0:COLS].indirect(T.off[:, LW * d + a:LW * d + b])

    for q in (v, sc):
        q.wait_ge(S.c3, 1)
        q.wait_ge(S.xin, 32)
    byv, bys = picks[rank]
    parts = {}
    for d, a, b in byv + bys:
        parts[d] = parts.get(d, 0) + 1
    for d, a, b in byv:
        v.tensor_copy(target(d, a, b), column(d, a, b)).then_inc(S["q%d" % d], 1)
    for d, a, b in bys:
        sc.activation(target(d, a, b), column(d, a, b), ActivationFunctionType.Copy,
                      bias=-0.0, scale=1.0).then_inc(S["q%d" % d], 1)

    sent = 0
    for call in calls[rank]:
        trs = []
        for d, tgt, slot, eng in call:
            g.wait_ge(S["q%d" % d], parts[d])
        for d, tgt, slot, eng in call:
            rid, pid, _se = topo.addr(tgt)
            out = T.land[:, CAP * rank:CAP * (rank + 1)] if slot is None else T["hold%d" % slot][:, :]
            sem = S["a%d" % rank] if slot is None else S["fed%d" % slot]
            src = T.snd[:, CAP * d:CAP * (d + 1)]
            sent += len(eng)
            if len(call) == 1:
                g.remote_dma(out, src, sem, S.sent, pid, rid, _mask(eng))
            else:
                trs.append(RemoteDMATransfer(dst_ids=[DstId(rid=rid, pnc=pid)], dma_engine_mask=_mask(eng),
                                             remote_sem=sem, src=src, dst=out))
        if trs:
            g.remote_dma_fused(trs, local_sem=S.sent)

    def store(q, r, done):
        q.dma_start(T.y[:, CAP * r:CAP * (r + 1)], T.land[:, CAP * r:CAP * (r + 1)]).then_inc(S[done], 16)

    nq = [nearq[rank][k] for k in sorted(nearq[rank])]
    cq = [crossq[rank][k] for k in sorted(crossq[rank])]
    g.sync.wait_ge(S["q%d" % rank], parts[rank])
    store(g.sync, rank, "stn")
    for r, cnt in nq + cq[:1]:
        g.sync.wait_ge(S["a%d" % r], cnt)
        store(g.sync, r, "stn")
    g.sync.wait_ge(S.stn, 16 * (len(nq) + 2))
    for r, cnt in cq[1:]:
        sc.wait_ge(S["a%d" % r], cnt)
        store(sc, r, "stc")
    sc.wait_ge(S.stc, 16 * (len(cq) - 1))
    g.wait_ge(S.sent, sent)
